import numpy as np, ml_dtypes
CORES = [2,34,66,98,130,162,194,226,258,290,322,354,386,418,450,482]
N = 16
VB, TK = 4, 128
def setup_inputs(rng):
    h = (rng.standard_normal((128, TK), dtype=np.float32) / 8).astype(ml_dtypes.bfloat16)
    return {"h": np.broadcast_to(h, (N, 128, TK)).copy(), "w": rng.standard_normal((N, 128, VB * 128), dtype=np.float32).astype(ml_dtypes.bfloat16)}
def setup_inputs_big(rng):
    d = setup_inputs(rng)
    for k in ("h", "w"): d[k] = (d[k].astype(np.float32) * 1024.0).astype(d[k].dtype)
    return d
def setup_inputs_small(rng):
    d = setup_inputs(rng)
    for k in ("h", "w"): d[k] = (d[k].astype(np.float32) * (1 / 1024.0)).astype(d[k].dtype)
    return d
def setup_inputs_apart(rng):
    d = setup_inputs(rng)
    f = (10.0 ** rng.permutation(np.linspace(-1.5, 1.5, N))).astype(np.float32).reshape(N, 1, 1)
    for k in ("w",): d[k] = (d[k].astype(np.float32) * f).astype(d[k].dtype)
    return d
def setup_inputs_neg(rng):
    d = setup_inputs(rng)
    d["h"] = (np.abs(d["h"].astype(np.float32)) * 1048576.0).astype(d["h"].dtype); d["w"] = (-np.abs(d["w"].astype(np.float32))).astype(d["w"].dtype)
    return d
def reference(h, w):
    H, W = h.astype(np.float64), w.astype(np.float64)
    Z = np.concatenate([W[r].T @ H[r] for r in range(N)], axis=0)
    m = Z.max(axis=0)
    s = np.maximum(Z - 0.5 * m, 0.0).sum(axis=0)
    return {"m": np.broadcast_to(m.astype(np.float32), (N, 1, TK)), "s": np.broadcast_to(s.astype(np.float32), (N, 1, TK))}

@@ -1,0 +1,178 @@
+from concourse.bass import DstId, RemoteDMATransfer
+from concourse.mybir import dt, AluOpType
+
+F, B = "float32", "bfloat16"
+SCRATCH = {
+    "hS": ("sbuf", [128, 128], B),
+    "wS": ("sbuf", [128, 512], B),
+    "A0": ("sbuf", [128, 129], B),
+    "Dd": ("dram", [129, 128], B),
+    "Ineg": ("sbuf", [128, 128], B),
+    "Z0": ("sbuf", [128, 128], F),
+    "on3": ("sbuf", [128, 128], B),
+    "on32": ("sbuf", [128, 4], F),
+    "tr": ("sbuf", [128, 768], F),
+    "LA": ("sbuf", [128, 16], F),
+    "LB": ("sbuf", [128, 16], F),
+    "LC": ("sbuf", [128, 16], F),
+    "LD": ("sbuf", [128, 16], F),
+    "sm": ("sbuf", [128, 96], F),
+    "mg": ("sbuf", [128, 4], F),
+    "sf": ("sbuf", [128, 4], F),
+    "C3": ("sbuf", [128, 8], B),
+    "rows3": ("sbuf", [128, 128], B),
+    "R": ("sbuf", [128, 512], F),
+    "zTa": ("psum", [128, 512], F),
+    "zTb": ("psum", [128, 512], F),
+    "z0": ("psum", [128, 512], F),
+    "z1": ("psum", [128, 512], F),
+    "z2": ("psum", [128, 512], F),
+    "z3": ("psum", [128, 512], F),
+}
+SEMAPHORES = ["a1", "a2", "a3", "a4", "sent"] + ["q%d" % i for i in range(64)]
+
+
+def _groups(core, cores, topo):
+    def idx(c):
+        return sorted(topo.chip(d) for d in cores if topo.host(d) == topo.host(c)).index(topo.chip(c))
+
+    def rk(c):
+        return topo.rack(topo.host(c))
+    ga = sorted(d for d in cores if rk(d) == rk(core) and idx(d) % 2 == idx(core) % 2)
+    gb = sorted(d for d in cores if idx(d) // 2 == idx(core) // 2 and
+                (topo.host(d) == topo.host(core) or (rk(d) != rk(core) and topo.may_write(core, d))))
+    return ga, gb
+
+
+def rank_program(g, core, T, topo):
+    if T.rank_of(core) is None:
+        return
+    V, P = g.vector, g.tensor
+    MAX, ADD, SUB = AluOpType.max, AluOpType.add, AluOpType.subtract
+    cnt = [0]
+
+    def new():
+        cnt[0] += 1
+        return T.sem["q%d" % (cnt[0] - 1)]
+
+    def vtt(out, a, b, op, waits):
+        for s, n in waits:
+            V.wait_ge(s, n)
+        s = new()
+        V.tensor_tensor(out, a, b, op).then_inc(s, 1)
+        return (s, 1)
+
+    def vcp(out, a, waits):
+        for s, n in waits:
+            V.wait_ge(s, n)
+        s = new()
+        V.tensor_copy(out, a).then_inc(s, 1)
+        return (s, 1)
+
+    ga, gb = _groups(core, T.cores, topo)
+    sent = [0]
+
+    def send(group, buf, sem, waits):
+        k = group.index(core)
+        ap = buf[:, 4 * k:4 * k + 4]
+        peers = [d for d in group if d != core]
+        mask = topo.mask(core, peers[0])
+        for d in peers:
+            mask &= topo.mask(core, d)
+        ids = []
+        for d in peers:
+            rid, pid = topo.addr(d, core)
+            ids.append(DstId(rid=rid, pnc=pid))
+        for s, n in waits:
+            g.wait_ge(s, n)
+        g.remote_dma_fused([RemoteDMATransfer(dst_ids=ids, dma_engine_mask=mask, remote_sem=sem, srcs=[ap],
+                                              dsts=[ap for _ in peers], alu_op=0)], local_sem=T.sem.sent)
+        ne = bin(mask).count("1")
+        sent[0] += ne
+        return (sem, ne * len(peers))
+
+    def slot(group, buf):
+        k = group.index(core)
+        return buf[:, 4 * k:4 * k + 4]
+
+    s_w, s_h, s_c, s_i1, s_i2 = new(), new(), new(), new(), new()
+    g.sync.dma_start(T.wS[:], T.w[:]).then_inc(s_w, 16)
+    g.scalar.dma_start(T.hS[:], T.h[:]).then_inc(s_h, 16)
+
+    V.memset(T.A0[:, 1:129], 0.0).then_inc(s_c, 1)
+    V.memset(T.A0[:, 0:1], -0.5).then_inc(s_c, 1)
+    V.memset(T.Z0[:], 0.0).then_inc(s_c, 1)
+    V.memset(T.on3[0:3, :], 1.0).then_inc(s_c, 1)
+    V.memset(T.on32[:], 1.0).then_inc(s_c, 1)
+    cst = (s_c, 5)
+    g.scalar.wait_ge(s_c, 5)
+    g.scalar.dma_start(T.Dd[:], T.A0[:]).then_inc(s_i1, 16)
+    g.scalar.wait_ge(s_i1, 16)
+    g.scalar.dma_start(T.Ineg[:], T.Dd[0:128, :]).then_inc(s_i2, 16)
+
+    zb = [T.z0, T.z1, T.z2, T.z3]
+    s_pa, s_pb = new(), new()
+    P.wait_ge(s_w, 16)
+    P.wait_ge(s_h, 16)
+    P.matmul(T.zTa[:, 0:256], T.hS[:], T.wS[:, 0:256], True, True).then_inc(s_pa, 1)
+    P.matmul(T.zTb[:, 0:256], T.hS[:], T.wS[:, 256:512], True, True).then_inc(s_pb, 1)
+    for b in range(4):
+        P.matmul(zb[b][:, 0:128], T.wS[:, 128 * b:128 * b + 128], T.hS[:], True, False)
+
+    tr = T.tr
+    d = vcp(tr[:, 0:256], T.zTa[:, 0:256], [(s_pa, 1)])
+    d = vtt(tr[:, 256:512], tr[:, 0:256], T.zTb[:, 0:256], MAX, [d, (s_pb, 1)])
+    off, wd = 256, 256
+    while wd > 8:
+        nxt = off + wd
+        d = vtt(tr[:, nxt:nxt + wd // 2], tr[:, off:off + wd // 2], tr[:, off + wd // 2:off + wd], MAX, [d])
+        off, wd = nxt, wd // 2
+    d = vtt(slot(ga, T.LA), tr[:, off:off + 4], tr[:, off + 4:off + 8], MAX, [d])
+
+    sm = T.sm
+
+    def exchange2(op, first, LX, LY, semx, semy, o):
+        arr = send(ga, LX, semx, [first])
+        e = vtt(sm[:, o:o + 8], LX[:, 0:8], LX[:, 8:16], op, [first, arr])
+        e = vtt(slot(gb, LY), sm[:, o:o + 4], sm[:, o + 4:o + 8], op, [e])
+        arr = send(gb, LY, semy, [e])
+        e = vtt(sm[:, o + 8:o + 16], LY[:, 0:8], LY[:, 8:16], op, [e, arr])
+        e = vtt(sm[:, o + 16:o + 20], sm[:, o + 8:o + 12], sm[:, o + 12:o + 16], op, [e])
+        e = vtt(sm[:, o + 20:o + 22], sm[:, o + 16:o + 18], sm[:, o + 18:o + 20], op, [e])
+        return e
+
+    d = exchange2(MAX, d, T.LA, T.LB, T.sem.a1, T.sem.a2, 0)
+    C3 = T.C3
+    d_mg = vtt(T.mg[:, 0:1], sm[:, 20:21], sm[:, 21:22], MAX, [d])
+    d_hi = vtt(C3[:, 0:1], sm[:, 20:21], sm[:, 21:22], MAX, [])
+    d_r1 = vtt(sm[:, 24:25], T.mg[:, 0:1], C3[:, 0:1], SUB, [d_mg, d_hi])
+    d_mid = vtt(C3[:, 1:2], T.mg[:, 0:1], C3[:, 0:1], SUB, [])
+    d_lo = vtt(C3[:, 2:3], sm[:, 24:25], C3[:, 1:2], SUB, [d_r1, d_mid])
+    s_mst, s_sst = new(), new()
+    g.scalar.wait_ge(*d_mg)
+    g.scalar.dma_start(T.m[:], T.mg[:, 0:1]).then_inc(s_mst, 16)
+
+    s_a = new()
+    for s, n in (d_hi, d_mid, d_lo, (s_i2, 16), cst):
+        P.wait_ge(s, n)
+    P.matmul(T.zTa[0:3, 0:128], C3[:, 0:3], T.Ineg[:], True, True).then_inc(s_a, 1)
+    d_b = vcp(T.rows3[0:3, :], T.zTa[0:3, 0:128], [(s_a, 1)])
+    P.wait_ge(*d_b)
+    s_z = [new() for _ in range(4)]
+    for b in range(4):
+        P.matmul(zb[b][:, 0:128], T.on3[0:3, :], T.rows3[0:3, :], False, True).then_inc(s_z[b], 1)
+    s_s = new()
+    for b in range(4):
+        e = vtt(T.R[:, 128 * b:128 * b + 128], zb[b][:, 0:128], T.Z0[:], MAX, [(s_z[b], 1)] + ([cst] if b == 0 else []))
+        P.wait_ge(*e)
+        P.matmul(T.zTb[:, b:b + 1], T.R[:, 128 * b:128 * b + 128], T.on32[:, 0:1], True, True).then_inc(s_s, 1)
+    d = vcp(slot(ga, T.LC), T.zTb[:, 0:4], [(s_s, 4)])
+
+    d = exchange2(ADD, d, T.LC, T.LD, T.sem.a3, T.sem.a4, 32)
+    d = vtt(T.sf[:, 0:1], sm[:, 52:53], sm[:, 53:54], ADD, [d])
+    g.sync.wait_ge(*d)
+    g.sync.dma_start(T.s[:], T.sf[:, 0:1]).then_inc(s_sst, 16)
+
+    g.wait_ge(T.sem.sent, sent[0])
+    g.wait_ge(s_mst, 16)
+    g.wait_ge(s_sst, 16)

@@ -1,35 +1,26 @@
 from concourse.bass import DstId, RemoteDMATransfer
-from concourse.mybir import dt, AluOpType
+from concourse.mybir import dt, AluOpType, AxisListType, ActivationFunctionType
 
 F, B = "float32", "bfloat16"
 SCRATCH = {
     "hS": ("sbuf", [128, 128], B),
+    "hh": ("sbuf", [128, 128], B),
     "wS": ("sbuf", [128, 512], B),
-    "A0": ("sbuf", [128, 129], B),
-    "Dd": ("dram", [129, 128], B),
-    "Ineg": ("sbuf", [128, 128], B),
-    "Z0": ("sbuf", [128, 128], F),
-    "on3": ("sbuf", [128, 128], B),
-    "on32": ("sbuf", [128, 4], F),
-    "tr": ("sbuf", [128, 768], F),
     "LA": ("sbuf", [128, 16], F),
-    "LB": ("sbuf", [128, 16], F),
+    "LB": ("sbuf", [128, 52], F),
     "LC": ("sbuf", [128, 16], F),
-    "LD": ("sbuf", [128, 16], F),
-    "sm": ("sbuf", [128, 96], F),
+    "LD": ("sbuf", [128, 52], F),
+    "bias": ("sbuf", [128, 4], F),
     "mg": ("sbuf", [128, 4], F),
     "sf": ("sbuf", [128, 4], F),
-    "C3": ("sbuf", [128, 8], B),
-    "rows3": ("sbuf", [128, 128], B),
     "R": ("sbuf", [128, 512], F),
-    "zTa": ("psum", [128, 512], F),
-    "zTb": ("psum", [128, 512], F),
     "z0": ("psum", [128, 512], F),
     "z1": ("psum", [128, 512], F),
     "z2": ("psum", [128, 512], F),
     "z3": ("psum", [128, 512], F),
 }
-SEMAPHORES = ["a1", "a2", "a3", "a4", "sent"] + ["q%d" % i for i in range(64)]
+SEMAPHORES = ["a1", "a2", "a3", "a4", "sent", "ldw", "ldh", "hok", "p0", "p1", "p2", "p3", "loc", "fa", "bok", "mok",
+              "act", "fc", "sok", "mst", "sst"]
 
 
 def _groups(core, cores, topo):
@@ -47,34 +38,16 @@ def _groups(core, cores, topo):
 def rank_program(g, core, T, topo):
     if T.rank_of(core) is None:
         return
-    V, P = g.vector, g.tensor
-    MAX, ADD, SUB = AluOpType.max, AluOpType.add, AluOpType.subtract
-    cnt = [0]
-
-    def new():
-        cnt[0] += 1
-        return T.sem["q%d" % (cnt[0] - 1)]
-
-    def vtt(out, a, b, op, waits):
-        for s, n in waits:
-            V.wait_ge(s, n)
-        s = new()
-        V.tensor_tensor(out, a, b, op).then_inc(s, 1)
-        return (s, 1)
-
-    def vcp(out, a, waits):
-        for s, n in waits:
-            V.wait_ge(s, n)
-        s = new()
-        V.tensor_copy(out, a).then_inc(s, 1)
-        return (s, 1)
-
+    V, P, S, Y = g.vector, g.tensor, g.scalar, g.sync
+    sem = T.sem
+    MAX, ADD, MULT = AluOpType.max, AluOpType.add, AluOpType.mult
+    X = AxisListType.X
     ga, gb = _groups(core, T.cores, topo)
+    ka = ga.index(core)
+    zb = [T.z0, T.z1, T.z2, T.z3]
     sent = [0]
 
-    def send(group, buf, sem, waits):
-        k = group.index(core)
-        ap = buf[:, 4 * k:4 * k + 4]
+    def send(group, src, dst_of, rsem):
         peers = [d for d in group if d != core]
         mask = topo.mask(core, peers[0])
         for d in peers:
@@ -83,96 +56,58 @@ def rank_program(g, core, T, topo):
         for d in peers:
             rid, pid = topo.addr(d, core)
             ids.append(DstId(rid=rid, pnc=pid))
-        for s, n in waits:
-            g.wait_ge(s, n)
-        g.remote_dma_fused([RemoteDMATransfer(dst_ids=ids, dma_engine_mask=mask, remote_sem=sem, srcs=[ap],
-                                              dsts=[ap for _ in peers], alu_op=0)], local_sem=T.sem.sent)
+        g.remote_dma_fused([RemoteDMATransfer(dst_ids=ids, dma_engine_mask=mask, remote_sem=rsem, srcs=[src],
+                                              dsts=[dst_of(d) for d in peers], alu_op=0)], local_sem=sem.sent)
         ne = bin(mask).count("1")
         sent[0] += ne
-        return (sem, ne * len(peers))
+        return ne * len(peers)
 
-    def slot(group, buf):
-        k = group.index(core)
-        return buf[:, 4 * k:4 * k + 4]
+    def allreduce(LX, LY, own_sem, own_n, semx, semy, fold_sem, op, out, out_sem, negate):
+        own = LX[:, 4 * ka:4 * ka + 4]
+        g.wait_ge(own_sem, own_n)
+        nx = send(ga, own, lambda d: own, semx)
+        g.wait_ge(semx, nx)
 
-    s_w, s_h, s_c, s_i1, s_i2 = new(), new(), new(), new(), new()
-    g.sync.dma_start(T.wS[:], T.w[:]).then_inc(s_w, 16)
-    g.scalar.dma_start(T.hS[:], T.h[:]).then_inc(s_h, 16)
+        def land(d):
+            p = [x for x in gb if x != d].index(core)
+            return LY[:, 16 * p:16 * p + 16]
+        ny = send(gb, LX[:, 0:16], land, semy)
+        V.wait_ge(own_sem, own_n)
+        V.wait_ge(semx, nx)
+        V.tensor_reduce(LY[:, 48:49], LX[:, 0:16], X, op).then_inc(fold_sem, 1)
+        V.wait_ge(fold_sem, 1)
+        V.wait_ge(semy, ny)
+        V.tensor_reduce(out, LY[:, 0:49], X, op, negate=negate).then_inc(out_sem, 1)
 
-    V.memset(T.A0[:, 1:129], 0.0).then_inc(s_c, 1)
-    V.memset(T.A0[:, 0:1], -0.5).then_inc(s_c, 1)
-    V.memset(T.Z0[:], 0.0).then_inc(s_c, 1)
-    V.memset(T.on3[0:3, :], 1.0).then_inc(s_c, 1)
-    V.memset(T.on32[:], 1.0).then_inc(s_c, 1)
-    cst = (s_c, 5)
-    g.scalar.wait_ge(s_c, 5)
-    g.scalar.dma_start(T.Dd[:], T.A0[:]).then_inc(s_i1, 16)
-    g.scalar.wait_ge(s_i1, 16)
-    g.scalar.dma_start(T.Ineg[:], T.Dd[0:128, :]).then_inc(s_i2, 16)
+    Y.dma_start(T.wS[:], T.w[:]).then_inc(sem.ldw, 16)
+    S.dma_start(T.hS[:], T.h[:]).then_inc(sem.ldh, 16)
+    V.wait_ge(sem.ldh, 16)
+    V.tensor_scalar(T.hh[:], T.hS[:], 0.5, None, MULT).then_inc(sem.hok, 1)
 
-    zb = [T.z0, T.z1, T.z2, T.z3]
-    s_pa, s_pb = new(), new()
-    P.wait_ge(s_w, 16)
-    P.wait_ge(s_h, 16)
-    P.matmul(T.zTa[:, 0:256], T.hS[:], T.wS[:, 0:256], True, True).then_inc(s_pa, 1)
-    P.matmul(T.zTb[:, 0:256], T.hS[:], T.wS[:, 256:512], True, True).then_inc(s_pb, 1)
+    P.wait_ge(sem.hok, 1)
+    P.wait_ge(sem.ldw, 16)
     for b in range(4):
-        P.matmul(zb[b][:, 0:128], T.wS[:, 128 * b:128 * b + 128], T.hS[:], True, False)
-
-    tr = T.tr
-    d = vcp(tr[:, 0:256], T.zTa[:, 0:256], [(s_pa, 1)])
-    d = vtt(tr[:, 256:512], tr[:, 0:256], T.zTb[:, 0:256], MAX, [d, (s_pb, 1)])
-    off, wd = 256, 256
-    while wd > 8:
-        nxt = off + wd
-        d = vtt(tr[:, nxt:nxt + wd // 2], tr[:, off:off + wd // 2], tr[:, off + wd // 2:off + wd], MAX, [d])
-        off, wd = nxt, wd // 2
-    d = vtt(slot(ga, T.LA), tr[:, off:off + 4], tr[:, off + 4:off + 8], MAX, [d])
-
-    sm = T.sm
-
-    def exchange2(op, first, LX, LY, semx, semy, o):
-        arr = send(ga, LX, semx, [first])
-        e = vtt(sm[:, o:o + 8], LX[:, 0:8], LX[:, 8:16], op, [first, arr])
-        e = vtt(slot(gb, LY), sm[:, o:o + 4], sm[:, o + 4:o + 8], op, [e])
-        arr = send(gb, LY, semy, [e])
-        e = vtt(sm[:, o + 8:o + 16], LY[:, 0:8], LY[:, 8:16], op, [e, arr])
-        e = vtt(sm[:, o + 16:o + 20], sm[:, o + 8:o + 12], sm[:, o + 12:o + 16], op, [e])
-        e = vtt(sm[:, o + 20:o + 22], sm[:, o + 16:o + 18], sm[:, o + 18:o + 20], op, [e])
-        return e
-
-    d = exchange2(MAX, d, T.LA, T.LB, T.sem.a1, T.sem.a2, 0)
-    C3 = T.C3
-    d_mg = vtt(T.mg[:, 0:1], sm[:, 20:21], sm[:, 21:22], MAX, [d])
-    d_hi = vtt(C3[:, 0:1], sm[:, 20:21], sm[:, 21:22], MAX, [])
-    d_r1 = vtt(sm[:, 24:25], T.mg[:, 0:1], C3[:, 0:1], SUB, [d_mg, d_hi])
-    d_mid = vtt(C3[:, 1:2], T.mg[:, 0:1], C3[:, 0:1], SUB, [])
-    d_lo = vtt(C3[:, 2:3], sm[:, 24:25], C3[:, 1:2], SUB, [d_r1, d_mid])
-    s_mst, s_sst = new(), new()
-    g.scalar.wait_ge(*d_mg)
-    g.scalar.dma_start(T.m[:], T.mg[:, 0:1]).then_inc(s_mst, 16)
-
-    s_a = new()
-    for s, n in (d_hi, d_mid, d_lo, (s_i2, 16), cst):
-        P.wait_ge(s, n)
-    P.matmul(T.zTa[0:3, 0:128], C3[:, 0:3], T.Ineg[:], True, True).then_inc(s_a, 1)
-    d_b = vcp(T.rows3[0:3, :], T.zTa[0:3, 0:128], [(s_a, 1)])
-    P.wait_ge(*d_b)
-    s_z = [new() for _ in range(4)]
+        P.matmul(zb[b][:, 0:128], T.hh[:], T.wS[:, 128 * b:128 * b + 128], True, True).then_inc(sem["p%d" % b], 1)
     for b in range(4):
-        P.matmul(zb[b][:, 0:128], T.on3[0:3, :], T.rows3[0:3, :], False, True).then_inc(s_z[b], 1)
-    s_s = new()
+        V.wait_ge(sem["p%d" % b], 1)
+        V.tensor_reduce(T.LA[:, 4 * ka + b:4 * ka + b + 1], zb[b][:, 0:128], X, MAX).then_inc(sem.loc, 1)
+
+    allreduce(T.LA, T.LB, sem.loc, 4, sem.a1, sem.a2, sem.fa, MAX, T.bias[:, 0:1], sem.bok, True)
+
+    S.wait_ge(sem.bok, 1)
     for b in range(4):
-        e = vtt(T.R[:, 128 * b:128 * b + 128], zb[b][:, 0:128], T.Z0[:], MAX, [(s_z[b], 1)] + ([cst] if b == 0 else []))
-        P.wait_ge(*e)
-        P.matmul(T.zTb[:, b:b + 1], T.R[:, 128 * b:128 * b + 128], T.on32[:, 0:1], True, True).then_inc(s_s, 1)
-    d = vcp(slot(ga, T.LC), T.zTb[:, 0:4], [(s_s, 4)])
+        S.activation(T.R[:, 128 * b:128 * b + 128], zb[b][:, 0:128], ActivationFunctionType.Relu, bias=T.bias[:, 0:1],
+                     scale=2.0, accum_out=T.LC[:, 4 * ka + b:4 * ka + b + 1]).then_inc(sem.act, 1)
 
-    d = exchange2(ADD, d, T.LC, T.LD, T.sem.a3, T.sem.a4, 32)
-    d = vtt(T.sf[:, 0:1], sm[:, 52:53], sm[:, 53:54], ADD, [d])
-    g.sync.wait_ge(*d)
-    g.sync.dma_start(T.s[:], T.sf[:, 0:1]).then_inc(s_sst, 16)
+    V.wait_ge(sem.bok, 1)
+    V.tensor_scalar(T.mg[:, 0:1], T.bias[:, 0:1], -2.0, None, MULT).then_inc(sem.mok, 1)
+    Y.wait_ge(sem.mok, 1)
+    Y.dma_start(T.m[:], T.mg[:, 0:1]).then_inc(sem.mst, 16)
 
-    g.wait_ge(T.sem.sent, sent[0])
-    g.wait_ge(s_mst, 16)
-    g.wait_ge(s_sst, 16)
+    allreduce(T.LC, T.LD, sem.act, 4, sem.a3, sem.a4, sem.fc, ADD, T.sf[:, 0:1], sem.sok, False)
+    Y.wait_ge(sem.sok, 1)
+    Y.dma_start(T.s[:], T.sf[:, 0:1]).then_inc(sem.sst, 16)
+
+    g.wait_ge(sem.sent, sent[0])
+    g.wait_ge(sem.mst, 16)
+    g.wait_ge(sem.sst, 16)

@@ -2,25 +2,30 @@ from concourse.bass import DstId, RemoteDMATransfer
 from concourse.mybir import dt, AluOpType, AxisListType, ActivationFunctionType
 
 F, B = "float32", "bfloat16"
+NS, NV = 384, 128
 SCRATCH = {
     "hS": ("sbuf", [128, 128], B),
-    "hh": ("sbuf", [128, 128], B),
+    "h2": ("sbuf", [128, 128], B),
     "wS": ("sbuf", [128, 512], B),
     "LA": ("sbuf", [128, 16], F),
     "LB": ("sbuf", [128, 52], F),
-    "LC": ("sbuf", [128, 16], F),
-    "LD": ("sbuf", [128, 52], F),
+    "LC": ("sbuf", [128, 12], F),
+    "LD": ("sbuf", [128, 28], F),
     "bias": ("sbuf", [128, 4], F),
     "mg": ("sbuf", [128, 4], F),
     "sf": ("sbuf", [128, 4], F),
-    "R": ("sbuf", [128, 512], F),
+    "R": ("sbuf", [128, NS], F),
+    "R2": ("sbuf", [128, NV], F),
+    "R3": ("sbuf", [128, 28], F),
     "z0": ("psum", [128, 512], F),
     "z1": ("psum", [128, 512], F),
     "z2": ("psum", [128, 512], F),
     "z3": ("psum", [128, 512], F),
+    "yS": ("psum", [128, 512], F),
+    "yV": ("psum", [128, 512], F),
 }
-SEMAPHORES = ["a1", "a2", "a3", "a4", "sent", "ldw", "ldh", "hok", "p0", "p1", "p2", "p3", "loc", "fa", "bok", "mok",
-              "act", "fc", "sok", "mst", "sst"]
+SEMAPHORES = ["a1", "a2", "a3", "a4", "sent", "ldw", "ldh", "h2ok", "p0", "p1", "p2", "p3", "py", "loc", "fa", "bok",
+              "mok", "vr", "act", "fc", "sok", "mst", "sst"]
 
 
 def _groups(core, cores, topo):
@@ -42,13 +47,26 @@ def rank_program(g, core, T, topo):
     sem = T.sem
     MAX, ADD, MULT = AluOpType.max, AluOpType.add, AluOpType.mult
     X = AxisListType.X
+    ACT = ActivationFunctionType
     ga, gb = _groups(core, T.cores, topo)
-    ka = ga.index(core)
     zb = [T.z0, T.z1, T.z2, T.z3]
     sent = [0]
 
+    def links(d):
+        n = 0
+        if topo.rack(topo.host(d)) != topo.rack(topo.host(core)):
+            n += 1
+            if topo.chip(d) != topo.chip(core):
+                n += 1
+        else:
+            n += 1
+        return n
+
+    def place(group, d):
+        return [x for x in group if x != d].index(core)
+
     def send(group, src, dst_of, rsem):
-        peers = [d for d in group if d != core]
+        peers = sorted((d for d in group if d != core), key=lambda d: (-links(d), d))
         mask = topo.mask(core, peers[0])
         for d in peers:
             mask &= topo.mask(core, d)
@@ -62,51 +80,61 @@ def rank_program(g, core, T, topo):
         sent[0] += ne
         return ne * len(peers)
 
-    def allreduce(LX, LY, own_sem, own_n, semx, semy, fold_sem, op, out, out_sem, negate):
-        own = LX[:, 4 * ka:4 * ka + 4]
+    def exchanges(LX, LY, k, own_sem, own_n, semx, semy, fold_sem, op):
+        own = LX[:, 4 - k:4]
         g.wait_ge(own_sem, own_n)
-        nx = send(ga, own, lambda d: own, semx)
+        nx = send(ga, own, lambda d: LX[:, 4 + k * place(ga, d):4 + k * place(ga, d) + k], semx)
         g.wait_ge(semx, nx)
-
-        def land(d):
-            p = [x for x in gb if x != d].index(core)
-            return LY[:, 16 * p:16 * p + 16]
-        ny = send(gb, LX[:, 0:16], land, semy)
+        row = LX[:, 4 - k:4 + 3 * k]
+        ny = send(gb, row, lambda d: LY[:, 4 * k * place(gb, d):4 * k * place(gb, d) + 4 * k], semy)
         V.wait_ge(own_sem, own_n)
         V.wait_ge(semx, nx)
-        V.tensor_reduce(LY[:, 48:49], LX[:, 0:16], X, op).then_inc(fold_sem, 1)
-        V.wait_ge(fold_sem, 1)
-        V.wait_ge(semy, ny)
-        V.tensor_reduce(out, LY[:, 0:49], X, op, negate=negate).then_inc(out_sem, 1)
+        V.tensor_reduce(LY[:, 12 * k:12 * k + 1], row, X, op).then_inc(fold_sem, 1)
+        return ny
 
     Y.dma_start(T.wS[:], T.w[:]).then_inc(sem.ldw, 16)
     S.dma_start(T.hS[:], T.h[:]).then_inc(sem.ldh, 16)
-    V.wait_ge(sem.ldh, 16)
-    V.tensor_scalar(T.hh[:], T.hS[:], 0.5, None, MULT).then_inc(sem.hok, 1)
+    S.wait_ge(sem.ldh, 16)
+    S.activation(T.h2[:], T.hS[:], ACT.Copy, scale=2.0).then_inc(sem.h2ok, 1)
 
-    P.wait_ge(sem.hok, 1)
+    P.wait_ge(sem.ldh, 16)
     P.wait_ge(sem.ldw, 16)
     for b in range(4):
-        P.matmul(zb[b][:, 0:128], T.hh[:], T.wS[:, 128 * b:128 * b + 128], True, True).then_inc(sem["p%d" % b], 1)
+        P.matmul(zb[b][:, 0:128], T.hS[:], T.wS[:, 128 * b:128 * b + 128], True, True).then_inc(sem["p%d" % b], 1)
     for b in range(4):
         V.wait_ge(sem["p%d" % b], 1)
-        V.tensor_reduce(T.LA[:, 4 * ka + b:4 * ka + b + 1], zb[b][:, 0:128], X, MAX).then_inc(sem.loc, 1)
+        V.tensor_reduce(T.LA[:, b:b + 1], zb[b][:, 0:128], X, MAX).then_inc(sem.loc, 1)
 
-    allreduce(T.LA, T.LB, sem.loc, 4, sem.a1, sem.a2, sem.fa, MAX, T.bias[:, 0:1], sem.bok, True)
+    P.wait_ge(sem.h2ok, 1)
+    P.matmul(T.yS[:, 0:NS], T.h2[:], T.wS[:, 0:NS], True, True).then_inc(sem.py, 1)
+    P.matmul(T.yV[:, 0:NV], T.h2[:], T.wS[:, NS:NS + NV], True, True).then_inc(sem.py, 1)
 
+    ny = exchanges(T.LA, T.LB, 4, sem.loc, 4, sem.a1, sem.a2, sem.fa, MAX)
+    V.wait_ge(sem.fa, 1)
+    V.wait_ge(sem.a2, ny)
+    V.tensor_reduce(T.bias[:, 0:1], T.LB[:, 0:49], X, MAX, negate=True).then_inc(sem.bok, 1)
+
+    S.wait_ge(sem.py, 2)
     S.wait_ge(sem.bok, 1)
-    for b in range(4):
-        S.activation(T.R[:, 128 * b:128 * b + 128], zb[b][:, 0:128], ActivationFunctionType.Relu, bias=T.bias[:, 0:1],
-                     scale=2.0, accum_out=T.LC[:, 4 * ka + b:4 * ka + b + 1]).then_inc(sem.act, 1)
-
+    S.activation(T.R[:], T.yS[:, 0:NS], ACT.Relu, bias=T.bias[:, 0:1], scale=1.0,
+                 accum_out=T.LC[:, 2:3]).then_inc(sem.act, 1)
+    V.wait_ge(sem.py, 2)
     V.wait_ge(sem.bok, 1)
-    V.tensor_scalar(T.mg[:, 0:1], T.bias[:, 0:1], -2.0, None, MULT).then_inc(sem.mok, 1)
-    Y.wait_ge(sem.mok, 1)
-    Y.dma_start(T.m[:], T.mg[:, 0:1]).then_inc(sem.mst, 16)
+    V.tensor_scalar(T.R2[:], T.yV[:, 0:NV], T.bias[:, 0:1], 0.0, ADD, MAX).then_inc(sem.vr, 1)
+    V.wait_ge(sem.vr, 1)
+    V.tensor_reduce(T.LC[:, 3:4], T.R2[:], X, ADD).then_inc(sem.act, 1)
+    V.tensor_scalar(T.mg[:, 0:1], T.bias[:, 0:1], -1.0, None, MULT).then_inc(sem.mok, 1)
 
-    allreduce(T.LC, T.LD, sem.act, 4, sem.a3, sem.a4, sem.fc, ADD, T.sf[:, 0:1], sem.sok, False)
-    Y.wait_ge(sem.sok, 1)
-    Y.dma_start(T.s[:], T.sf[:, 0:1]).then_inc(sem.sst, 16)
+    ny = exchanges(T.LC, T.LD, 2, sem.act, 2, sem.a3, sem.a4, sem.fc, ADD)
+    S.wait_ge(sem.fc, 1)
+    S.wait_ge(sem.a4, ny)
+    S.activation(T.R3[:, 0:25], T.LD[:, 0:25], ACT.Copy, scale=0.5, accum_out=T.sf[:, 0:1]).then_inc(sem.sok, 1)
+    S.wait_ge(sem.sok, 1)
+    S.dma_start(T.s[:], T.sf[:, 0:1]).then_inc(sem.sst, 16)
+
+    Y.wait_ge(sem.mok, 1)
+    Y.wait_ge(sem.sent, sent[0])
+    Y.dma_start(T.m[:], T.mg[:, 0:1]).then_inc(sem.mst, 16)
 
     g.wait_ge(sem.sent, sent[0])
     g.wait_ge(sem.mst, 16)

@@ -2,30 +2,34 @@ from concourse.bass import DstId, RemoteDMATransfer
 from concourse.mybir import dt, AluOpType, AxisListType, ActivationFunctionType
 
 F, B = "float32", "bfloat16"
-NS, NV = 384, 128
+NW = 512
+W1 = 32
+NS2, NV = 192, 320
 SCRATCH = {
     "hS": ("sbuf", [128, 128], B),
     "h2": ("sbuf", [128, 128], B),
-    "wS": ("sbuf", [128, 512], B),
+    "wS": ("sbuf", [128, NW], B),
+    "wP": ("sbuf", [128, NW], B),
     "LA": ("sbuf", [128, 16], F),
     "LB": ("sbuf", [128, 52], F),
-    "LC": ("sbuf", [128, 12], F),
-    "LD": ("sbuf", [128, 28], F),
+    "LC": ("sbuf", [128, 28], F),
     "bias": ("sbuf", [128, 4], F),
     "mg": ("sbuf", [128, 4], F),
     "sf": ("sbuf", [128, 4], F),
-    "R": ("sbuf", [128, NS], F),
+    "R": ("sbuf", [128, NW], F),
+    "Rb": ("sbuf", [128, NS2], F),
     "R2": ("sbuf", [128, NV], F),
     "R3": ("sbuf", [128, 28], F),
     "z0": ("psum", [128, 512], F),
     "z1": ("psum", [128, 512], F),
     "z2": ("psum", [128, 512], F),
     "z3": ("psum", [128, 512], F),
-    "yS": ("psum", [128, 512], F),
-    "yV": ("psum", [128, 512], F),
+    "yA": ("psum", [128, 512], F),
+    "yB": ("psum", [128, 512], F),
+    "yC": ("psum", [128, 512], F),
 }
-SEMAPHORES = ["a1", "a2", "a3", "a4", "sent", "ldw", "ldh", "h2ok", "p0", "p1", "p2", "p3", "py", "loc", "fa", "bok",
-              "mok", "vr", "act", "fc", "sok", "mst", "sst"]
+SEMAPHORES = ["a1", "a2", "a3", "wp", "sent", "ldw", "ldh", "h2ok", "p0", "p1", "p2", "p3", "py", "loc", "fa", "bok",
+              "mok", "vr", "act", "sok", "mst", "sst"]
 
 
 def _groups(core, cores, topo):
@@ -34,10 +38,14 @@ def _groups(core, cores, topo):
 
     def rk(c):
         return topo.rack(topo.host(c))
+
+    def near(d):
+        return topo.host(d) == topo.host(core) or (rk(d) != rk(core) and topo.may_write(core, d))
     ga = sorted(d for d in cores if rk(d) == rk(core) and idx(d) % 2 == idx(core) % 2)
-    gb = sorted(d for d in cores if idx(d) // 2 == idx(core) // 2 and
-                (topo.host(d) == topo.host(core) or (rk(d) != rk(core) and topo.may_write(core, d))))
-    return ga, gb
+    gb = sorted(d for d in cores if idx(d) // 2 == idx(core) // 2 and near(d))
+    gc = sorted(d for d in cores if near(d))
+    partner = [d for d in cores if d != core and topo.same_plane(core, d) and topo.chip(d) == topo.chip(core)][0]
+    return ga, gb, gc, partner
 
 
 def rank_program(g, core, T, topo):
@@ -48,7 +56,7 @@ def rank_program(g, core, T, topo):
     MAX, ADD, MULT = AluOpType.max, AluOpType.add, AluOpType.mult
     X = AxisListType.X
     ACT = ActivationFunctionType
-    ga, gb = _groups(core, T.cores, topo)
+    ga, gb, gc, partner = _groups(core, T.cores, topo)
     zb = [T.z0, T.z1, T.z2, T.z3]
     sent = [0]
 
@@ -80,22 +88,13 @@ def rank_program(g, core, T, topo):
         sent[0] += ne
         return ne * len(peers)
 
-    def exchanges(LX, LY, k, own_sem, own_n, semx, semy, fold_sem, op):
-        own = LX[:, 4 - k:4]
-        g.wait_ge(own_sem, own_n)
-        nx = send(ga, own, lambda d: LX[:, 4 + k * place(ga, d):4 + k * place(ga, d) + k], semx)
-        g.wait_ge(semx, nx)
-        row = LX[:, 4 - k:4 + 3 * k]
-        ny = send(gb, row, lambda d: LY[:, 4 * k * place(gb, d):4 * k * place(gb, d) + 4 * k], semy)
-        V.wait_ge(own_sem, own_n)
-        V.wait_ge(semx, nx)
-        V.tensor_reduce(LY[:, 12 * k:12 * k + 1], row, X, op).then_inc(fold_sem, 1)
-        return ny
-
     Y.dma_start(T.wS[:], T.w[:]).then_inc(sem.ldw, 16)
     S.dma_start(T.hS[:], T.h[:]).then_inc(sem.ldh, 16)
     S.wait_ge(sem.ldh, 16)
     S.activation(T.h2[:], T.hS[:], ACT.Copy, scale=2.0).then_inc(sem.h2ok, 1)
+
+    g.wait_ge(sem.ldw, 16)
+    nw = send([core, partner], T.wS[:, 0:W1], lambda d: T.wP[:, 0:W1], sem.wp)
 
     P.wait_ge(sem.ldh, 16)
     P.wait_ge(sem.ldw, 16)
@@ -105,30 +104,43 @@ def rank_program(g, core, T, topo):
         V.wait_ge(sem["p%d" % b], 1)
         V.tensor_reduce(T.LA[:, b:b + 1], zb[b][:, 0:128], X, MAX).then_inc(sem.loc, 1)
 
-    P.wait_ge(sem.h2ok, 1)
-    P.matmul(T.yS[:, 0:NS], T.h2[:], T.wS[:, 0:NS], True, True).then_inc(sem.py, 1)
-    P.matmul(T.yV[:, 0:NV], T.h2[:], T.wS[:, NS:NS + NV], True, True).then_inc(sem.py, 1)
+    g.wait_ge(sem.loc, 4)
+    nx = send(ga, T.LA[:, 0:4], lambda d: T.LA[:, 4 + 4 * place(ga, d):8 + 4 * place(ga, d)], sem.a1)
+    nw += send([core, partner], T.wS[:, W1:NW], lambda d: T.wP[:, W1:NW], sem.wp)
+    g.wait_ge(sem.a1, nx)
+    ny = send(gb, T.LA[:, 0:16], lambda d: T.LB[:, 16 * place(gb, d):16 * place(gb, d) + 16], sem.a2)
 
-    ny = exchanges(T.LA, T.LB, 4, sem.loc, 4, sem.a1, sem.a2, sem.fa, MAX)
+    P.wait_ge(sem.h2ok, 1)
+    P.matmul(T.yA[:, 0:NW], T.h2[:], T.wS[:], True, True).then_inc(sem.py, 1)
+    P.wait_ge(sem.wp, nw)
+    P.matmul(T.yB[:, 0:NS2], T.h2[:], T.wP[:, 0:NS2], True, True).then_inc(sem.py, 1)
+    P.matmul(T.yC[:, 0:NV], T.h2[:], T.wP[:, NS2:NS2 + NV], True, True).then_inc(sem.py, 1)
+
+    V.wait_ge(sem.loc, 4)
+    V.wait_ge(sem.a1, nx)
+    V.tensor_reduce(T.LB[:, 48:49], T.LA[:, 0:16], X, MAX).then_inc(sem.fa, 1)
     V.wait_ge(sem.fa, 1)
     V.wait_ge(sem.a2, ny)
     V.tensor_reduce(T.bias[:, 0:1], T.LB[:, 0:49], X, MAX, negate=True).then_inc(sem.bok, 1)
 
-    S.wait_ge(sem.py, 2)
+    S.wait_ge(sem.py, 3)
     S.wait_ge(sem.bok, 1)
-    S.activation(T.R[:], T.yS[:, 0:NS], ACT.Relu, bias=T.bias[:, 0:1], scale=1.0,
+    S.activation(T.R[:], T.yA[:, 0:NW], ACT.Relu, bias=T.bias[:, 0:1], scale=1.0,
+                 accum_out=T.LC[:, 1:2]).then_inc(sem.act, 1)
+    S.activation(T.Rb[:], T.yB[:, 0:NS2], ACT.Relu, bias=T.bias[:, 0:1], scale=1.0,
                  accum_out=T.LC[:, 2:3]).then_inc(sem.act, 1)
-    V.wait_ge(sem.py, 2)
+    V.wait_ge(sem.py, 3)
     V.wait_ge(sem.bok, 1)
-    V.tensor_scalar(T.R2[:], T.yV[:, 0:NV], T.bias[:, 0:1], 0.0, ADD, MAX).then_inc(sem.vr, 1)
+    V.tensor_scalar(T.R2[:], T.yC[:, 0:NV], T.bias[:, 0:1], 0.0, ADD, MAX).then_inc(sem.vr, 1)
     V.wait_ge(sem.vr, 1)
     V.tensor_reduce(T.LC[:, 3:4], T.R2[:], X, ADD).then_inc(sem.act, 1)
     V.tensor_scalar(T.mg[:, 0:1], T.bias[:, 0:1], -1.0, None, MULT).then_inc(sem.mok, 1)
 
-    ny = exchanges(T.LC, T.LD, 2, sem.act, 2, sem.a3, sem.a4, sem.fc, ADD)
-    S.wait_ge(sem.fc, 1)
-    S.wait_ge(sem.a4, ny)
-    S.activation(T.R3[:, 0:25], T.LD[:, 0:25], ACT.Copy, scale=0.5, accum_out=T.sf[:, 0:1]).then_inc(sem.sok, 1)
+    g.wait_ge(sem.act, 3)
+    nc = send(gc, T.LC[:, 1:4], lambda d: T.LC[:, 4 + 3 * place(gc, d):7 + 3 * place(gc, d)], sem.a3)
+    S.wait_ge(sem.act, 3)
+    S.wait_ge(sem.a3, nc)
+    S.activation(T.R3[:, 0:24], T.LC[:, 1:25], ACT.Copy, scale=0.5, accum_out=T.sf[:, 0:1]).then_inc(sem.sok, 1)
     S.wait_ge(sem.sok, 1)
     S.dma_start(T.s[:], T.sf[:, 0:1]).then_inc(sem.sst, 16)
 

from concourse.bass import DstId, RemoteDMATransfer
from concourse.mybir import dt, AluOpType, AxisListType, ActivationFunctionType

F, B = "float32", "bfloat16"
NW = 512
W1 = 32
NS2, NV = 192, 320
SCRATCH = {
    "hS": ("sbuf", [128, 128], B),
    "h2": ("sbuf", [128, 128], B),
    "wS": ("sbuf", [128, NW], B),
    "wP": ("sbuf", [128, NW], B),
    "LA": ("sbuf", [128, 16], F),
    "LB": ("sbuf", [128, 52], F),
    "LC": ("sbuf", [128, 28], F),
    "bias": ("sbuf", [128, 4], F),
    "mg": ("sbuf", [128, 4], F),
    "sf": ("sbuf", [128, 4], F),
    "R": ("sbuf", [128, NW], F),
    "Rb": ("sbuf", [128, NS2], F),
    "R2": ("sbuf", [128, NV], F),
    "R3": ("sbuf", [128, 28], F),
    "z0": ("psum", [128, 512], F),
    "z1": ("psum", [128, 512], F),
    "z2": ("psum", [128, 512], F),
    "z3": ("psum", [128, 512], F),
    "yA": ("psum", [128, 512], F),
    "yB": ("psum", [128, 512], F),
    "yC": ("psum", [128, 512], F),
}
SEMAPHORES = ["a1", "a2", "a3", "wp", "sent", "ldw", "ldh", "h2ok", "p0", "p1", "p2", "p3", "py", "loc", "fa", "bok",
              "mok", "vr", "act", "sok", "mst", "sst"]


def _groups(core, cores, topo):
    def idx(c):
        return sorted(topo.chip(d) for d in cores if topo.host(d) == topo.host(c)).index(topo.chip(c))

    def rk(c):
        return topo.rack(topo.host(c))

    def near(d):
        return topo.host(d) == topo.host(core) or (rk(d) != rk(core) and topo.may_write(core, d))
    ga = sorted(d for d in cores if rk(d) == rk(core) and idx(d) % 2 == idx(core) % 2)
    gb = sorted(d for d in cores if idx(d) // 2 == idx(core) // 2 and near(d))
    gc = sorted(d for d in cores if near(d))
    partner = [d for d in cores if d != core and topo.same_plane(core, d) and topo.chip(d) == topo.chip(core)][0]
    return ga, gb, gc, partner


def rank_program(g, core, T, topo):
    if T.rank_of(core) is None:
        return
    V, P, S, Y = g.vector, g.tensor, g.scalar, g.sync
    sem = T.sem
    MAX, ADD, MULT = AluOpType.max, AluOpType.add, AluOpType.mult
    X = AxisListType.X
    ACT = ActivationFunctionType
    ga, gb, gc, partner = _groups(core, T.cores, topo)
    zb = [T.z0, T.z1, T.z2, T.z3]
    sent = [0]

    def links(d):
        n = 0
        if topo.rack(topo.host(d)) != topo.rack(topo.host(core)):
            n += 1
            if topo.chip(d) != topo.chip(core):
                n += 1
        else:
            n += 1
        return n

    def place(group, d):
        return [x for x in group if x != d].index(core)

    def send(group, src, dst_of, rsem):
        peers = sorted((d for d in group if d != core), key=lambda d: (-links(d), d))
        mask = topo.mask(core, peers[0])
        for d in peers:
            mask &= topo.mask(core, d)
        ids = []
        for d in peers:
            rid, pid = topo.addr(d, core)
            ids.append(DstId(rid=rid, pnc=pid))
        g.remote_dma_fused([RemoteDMATransfer(dst_ids=ids, dma_engine_mask=mask, remote_sem=rsem, srcs=[src],
                                              dsts=[dst_of(d) for d in peers], alu_op=0)], local_sem=sem.sent)
        ne = bin(mask).count("1")
        sent[0] += ne
        return ne * len(peers)

    Y.dma_start(T.wS[:], T.w[:]).then_inc(sem.ldw, 16)
    S.dma_start(T.hS[:], T.h[:]).then_inc(sem.ldh, 16)
    S.wait_ge(sem.ldh, 16)
    S.activation(T.h2[:], T.hS[:], ACT.Copy, scale=2.0).then_inc(sem.h2ok, 1)

    g.wait_ge(sem.ldw, 16)
    nw = send([core, partner], T.wS[:, 0:W1], lambda d: T.wP[:, 0:W1], sem.wp)

    P.wait_ge(sem.ldh, 16)
    P.wait_ge(sem.ldw, 16)
    for b in range(4):
        P.matmul(zb[b][:, 0:128], T.hS[:], T.wS[:, 128 * b:128 * b + 128], True, True).then_inc(sem["p%d" % b], 1)
    for b in range(4):
        V.wait_ge(sem["p%d" % b], 1)
        V.tensor_reduce(T.LA[:, b:b + 1], zb[b][:, 0:128], X, MAX).then_inc(sem.loc, 1)

    g.wait_ge(sem.loc, 4)
    nx = send(ga, T.LA[:, 0:4], lambda d: T.LA[:, 4 + 4 * place(ga, d):8 + 4 * place(ga, d)], sem.a1)
    nw += send([core, partner], T.wS[:, W1:NW], lambda d: T.wP[:, W1:NW], sem.wp)
    g.wait_ge(sem.a1, nx)
    ny = send(gb, T.LA[:, 0:16], lambda d: T.LB[:, 16 * place(gb, d):16 * place(gb, d) + 16], sem.a2)

    P.wait_ge(sem.h2ok, 1)
    P.matmul(T.yA[:, 0:NW], T.h2[:], T.wS[:], True, True).then_inc(sem.py, 1)
    P.wait_ge(sem.wp, nw)
    P.matmul(T.yB[:, 0:NS2], T.h2[:], T.wP[:, 0:NS2], True, True).then_inc(sem.py, 1)
    P.matmul(T.yC[:, 0:NV], T.h2[:], T.wP[:, NS2:NS2 + NV], True, True).then_inc(sem.py, 1)

    V.wait_ge(sem.loc, 4)
    V.wait_ge(sem.a1, nx)
    V.tensor_reduce(T.LB[:, 48:49], T.LA[:, 0:16], X, MAX).then_inc(sem.fa, 1)
    V.wait_ge(sem.fa, 1)
    V.wait_ge(sem.a2, ny)
    V.tensor_reduce(T.bias[:, 0:1], T.LB[:, 0:49], X, MAX, negate=True).then_inc(sem.bok, 1)

    S.wait_ge(sem.py, 3)
    S.wait_ge(sem.bok, 1)
    S.activation(T.R[:], T.yA[:, 0:NW], ACT.Relu, bias=T.bias[:, 0:1], scale=1.0,
                 accum_out=T.LC[:, 1:2]).then_inc(sem.act, 1)
    S.activation(T.Rb[:], T.yB[:, 0:NS2], ACT.Relu, bias=T.bias[:, 0:1], scale=1.0,
                 accum_out=T.LC[:, 2:3]).then_inc(sem.act, 1)
    V.wait_ge(sem.py, 3)
    V.wait_ge(sem.bok, 1)
    V.tensor_scalar(T.R2[:], T.yC[:, 0:NV], T.bias[:, 0:1], 0.0, ADD, MAX).then_inc(sem.vr, 1)
    V.wait_ge(sem.vr, 1)
    V.tensor_reduce(T.LC[:, 3:4], T.R2[:], X, ADD).then_inc(sem.act, 1)
    V.tensor_scalar(T.mg[:, 0:1], T.bias[:, 0:1], -1.0, None, MULT).then_inc(sem.mok, 1)

    g.wait_ge(sem.act, 3)
    nc = send(gc, T.LC[:, 1:4], lambda d: T.LC[:, 4 + 3 * place(gc, d):7 + 3 * place(gc, d)], sem.a3)
    S.wait_ge(sem.act, 3)
    S.wait_ge(sem.a3, nc)
    S.activation(T.R3[:, 0:24], T.LC[:, 1:25], ACT.Copy, scale=0.5, accum_out=T.sf[:, 0:1]).then_inc(sem.sok, 1)
    S.wait_ge(sem.sok, 1)
    S.dma_start(T.s[:], T.sf[:, 0:1]).then_inc(sem.sst, 16)

    Y.wait_ge(sem.mok, 1)
    Y.wait_ge(sem.sent, sent[0])
    Y.dma_start(T.m[:], T.mg[:, 0:1]).then_inc(sem.mst, 16)

    g.wait_ge(sem.sent, sent[0])
    g.wait_ge(sem.mst, 16)
    g.wait_ge(sem.sst, 16)
